import numpy as np
import ml_dtypes


def mxq(x, axis, fmt="e4m3"):
    dtype, down = {"e4m3": (ml_dtypes.float8_e4m3fn, 7), "e5m2": (ml_dtypes.float8_e5m2, 14)}[fmt]
    v = np.moveaxis(np.asarray(x, np.float32).astype(ml_dtypes.bfloat16).astype(np.float64), axis, -1)
    blocks = v.reshape(v.shape[:-1] + (-1, 32))
    amax = np.abs(blocks).max(-1, keepdims=True)
    byte = np.maximum(np.where(amax > 0, np.frexp(amax)[1] - 1 + 127, 0) - down, 1)
    scale = np.exp2(byte - 127.0)
    codes = (blocks / scale).astype(np.float32).astype(dtype).astype(np.float64)
    return np.moveaxis((codes * scale).reshape(v.shape), -1, axis)


WIDE = False


def mx_kscale(k):
    if not WIDE:
        return np.ones(k)
    levels = np.array([10, -10, 5, -5, 0])
    if k % 512:
        return np.exp2(np.random.permutation(np.resize(levels, k // 32))).repeat(32)
    a = np.empty((k // 512, 16))
    for p in range(k // 512):
        a[p, :8] = np.random.permutation(np.resize(levels, 8))
        for g in range(8):
            far = levels[np.abs(levels - a[p, g]) >= 10]
            a[p, g + 8] = far[np.random.randint(len(far))]
    return np.exp2(a.ravel()).repeat(32)


def f64(x):
    return np.asarray(x).astype(np.float64)


def striped(idx):
    return np.tile(idx.reshape(-1, 16).T, (8, 1)).astype(np.uint16)


def unstriped(offs):
    return offs[:16].T.reshape(-1).astype(np.int64)


E2M1 = np.array([0.0, 0.5, 1.0, 1.5, 2.0, 3.0, 4.0, 6.0, -0.0, -0.5, -1.0, -1.5, -2.0, -3.0, -4.0, -6.0])


def pack_weight(w, fmt):
    k, n = w.shape
    w = f64(np.asarray(w, np.float32).astype(ml_dtypes.bfloat16)).reshape(k // 32, 32, n)
    amax = np.abs(w).max(1)
    if fmt == "e4m3":
        byte = np.frexp(amax)[1] - 1 + 127 - 7
    else:
        mant, ex = np.frexp(amax / 6.0)
        byte = np.where(mant > 0.5, ex, ex - 1) + 127
    byte = np.clip(np.where(amax > 0, byte, 1), 1, 254)
    scaled = (w * np.exp2(127.0 - byte)[:, None, :]).reshape(k, n).astype(np.float32)
    by_word = np.ascontiguousarray(scaled.reshape(k // 512, 128, 4, n).transpose(0, 1, 3, 2))
    if fmt == "e4m3":
        words = by_word.astype(ml_dtypes.float8_e4m3fn).view(np.uint8)
    else:
        c = by_word.astype(ml_dtypes.float4_e2m1fn).view(np.uint8) & 0xF
        words = (c[..., 0::2] | (c[..., 1::2] << 4)).reshape(k // 512, 128, 2 * n)
    return np.ascontiguousarray(words), np.ascontiguousarray(byte.astype(np.uint8).reshape(k // 512, 16, n))


def unpack_weight(words, scales, fmt):
    g, _, n = scales.shape
    words = np.ascontiguousarray(words).reshape(g, 128, n, -1)
    if fmt == "e4m3":
        vals = words.view(ml_dtypes.float8_e4m3fn).astype(np.float64)
    else:
        nib = np.empty((g, 128, n, 4), np.uint8)
        nib[..., 0::2] = words & 0xF
        nib[..., 1::2] = words >> 4
        vals = E2M1[nib]
    vals = vals * np.repeat(np.exp2(scales.astype(np.float64) - 127.0), 8, axis=1)[..., None]
    return vals.transpose(0, 1, 3, 2).reshape(g * 512, n)


def gelu(v):
    return 0.5 * v * (1.0 + np.tanh(np.sqrt(2.0 / np.pi) * (v + 0.044715 * v**3)))


K, H, T, S, T2, P = 512, 1024, 2048, 512, 1024, 512

def setup_inputs():
    n = np.random.standard_normal
    s = mx_kscale(K)[:, None]
    u = mx_kscale(H)[:, None]
    d = {}
    d["tab_words"], d["tab_scales"] = pack_weight(n((K, T)) * s, "e4m3")
    d["w1"] = (1.1 * n((K, H)) / K ** 0.5 / s).astype(np.float32)
    d["w2_words"], d["w2_scales"] = pack_weight(1.6 * n((H, H)) / H ** 0.5 / u, "e2m1")
    d["w3"] = (1.2 * n((H, H)) / H ** 0.5 / u).astype(np.float32)
    d["gain1"] = (np.random.uniform(0.7, 1.4, H) * u[:, 0]).astype(np.float32)
    d["gain2"] = (np.random.uniform(0.7, 1.4, H) * u[:, 0]).astype(np.float32)
    d["base"] = np.random.uniform(0.7, 1.4, H).astype(np.float32)
    d["page0"] = np.random.uniform(-1.8, 1.8, (H, T2)).astype(np.float32)
    d["wgs"] = (0.22 * np.exp(0.3 * np.clip(n((128, S)), -1.5, 1.5))).astype(np.float32)
    d["offs"] = striped(np.random.permutation(T)[:S])
    d["offs2"] = striped(np.random.permutation(T2)[:S])
    d["offs3"] = striped(np.random.permutation(T2)[:P])
    d["offs4"] = striped(np.random.permutation(T2)[:P])
    return d

def reference(tab_words, tab_scales, w1, w2_words, w2_scales, w3, gain1, gain2, base, page0, wgs, offs, offs2, offs3, offs4):
    v = unpack_weight(tab_words, tab_scales, "e4m3")[:, unstriped(offs)]
    w1q = mxq(f64(w1), 0, "e4m3")
    w2 = unpack_weight(w2_words, w2_scales, "e2m1")
    a = w1q.T @ v
    gelu = 0.5 * a * (1.0 + np.tanh(0.7978845608 * (a + 0.044715 * a ** 3)))
    b = mxq(gelu * f64(gain1)[:, None], 0, "e4m3")
    h = w2.T @ b + w1q.T @ v
    page = f64(page0).copy()
    page[:, unstriped(offs2)] = np.tile(f64(wgs), (H // 128, 1)) * h
    x = np.cos(page[:, unstriped(offs3)]) * f64(gain2)[:, None]
    y = mxq(f64(w3), 0, "e4m3").T @ mxq(x, 0, "e4m3")
    ref = page[:, unstriped(offs4)] * f64(base)[:, None]
    return np.square(y - ref)

@@ -1,0 +1,264 @@
+import math
+from contextlib import ExitStack
+
+import concourse.mybir as mybir
+
+K, H, T, S, T2, NP = 512, 1024, 2048, 512, 1024, 512
+FLOPS = 2 * (2 * K * H * S + H * H * S + H * H * NP)
+
+F32 = mybir.dt.float32
+BF16 = mybir.dt.bfloat16
+I32 = mybir.dt.int32
+U32 = mybir.dt.uint32
+U16 = mybir.dt.uint16
+U8 = mybir.dt.uint8
+FP8X4 = mybir.dt.float8_e4m3fn_x4
+FP4X4 = mybir.dt.float4_e2m1fn_x4
+ACT = mybir.ActivationFunctionType
+ALU = mybir.AluOpType
+
+P = 128
+PACK = 4
+PASS = P * PACK
+HALF = S // 2
+QUART = P
+
+
+def tile_list_epoch_baseline_contrast_kernel(
+    tc, tab_words, tab_scales, w1, w2_words, w2_scales, w3, gain1, gain2, base, page0, wgs,
+    offs, offs2, offs3, offs4, out,
+):
+    nc = tc.nc
+    slices = [(b, t) for b in range(2) for t in range(PACK)]
+
+    with ExitStack() as ctx:
+        keep = ctx.enter_context(tc.tile_pool(name="keep", bufs=1))
+        psum = ctx.enter_context(tc.psum_pool(name="psum", bufs=8))
+
+        def sb(name, shape, dtype, tag=""):
+            return keep.tile(shape, dtype, name=name, tag=tag or name, align_bytes=64)
+
+        def bank(shape):
+            return psum.tile(shape, F32, name="bank")
+
+        def quantize(codes, scales, src):
+            nc.vector.quantize_mx(out=codes.bitcast(FP8X4), scales=scales, in_=src)
+
+        lists = [keep.tile([P, S // 16], U16, name="list%d" % i) for i in range(4)]
+
+        w2_raw = sb("w2_raw", [P, 2, 2 * H], U8)
+        w2s_raw = sb("w2s_raw", [P, 2, H], U8)
+        tabw = sb("tabw", [P, T], I32)
+        tabs = sb("tabs", [P, T], U8)
+        warm = sb("warm", [P, 4], F32)
+        nc.vector.memset(w2s_raw[:, 0, :].bitcast(I32), 0)
+        nc.gpsimd.memset(w2s_raw[:, 1, :].bitcast(I32), 0)
+        nc.vector.memset(warm[:, 0:1], 0.0)
+        nc.scalar.activation(out=warm[:, 1:2], in_=warm[:, 0:1], func=ACT.Gelu_apprx_tanh)
+        g1 = sb("g1", [P, 2, PACK], F32)
+        g2 = sb("g2", [P, 2, PACK], F32)
+        bs = sb("bs", [P, 2, PACK], F32)
+
+        def load_vector(tile, vec):
+            nc.sync.dma_start(out=tile[:], in_=vec.rearrange("(b p t) -> p b t", b=2, t=PACK))
+
+        nc.sync.dma_start(out=w2_raw[:].bitcast(I32), in_=w2_words.rearrange("a p n -> p a n").bitcast(I32))
+        nc.sync.dma_start(lists[0][:], offs)
+        for q in range(4):
+            rows = tab_scales[0, 4 * q : 4 * q + 4, :].bitcast(I32)
+            nc.sync.dma_start(out=tabs[32 * q : 32 * q + 32, :].bitcast(I32),
+                              in_=rows.unsqueeze(0).to_broadcast([8, 4, T // 4]))
+        nc.sync.dma_start(out=tabw[:], in_=tab_words[0].rearrange("p n i -> p (n i)").bitcast(I32))
+        for q in range(4):
+            nc.sync.dma_start(out=w2s_raw[32 * q : 32 * q + 4, :, :].bitcast(I32),
+                              in_=w2_scales[:, 4 * q : 4 * q + 4, :].rearrange("a r n -> r a n").bitcast(I32))
+        w1_rows = w1.rearrange("(p i) c -> p i c", i=PACK)
+        w1_cols = [(c, c + 256) for c in range(0, H, 256)]
+        w1_raw = []
+        for n, (c0, c1) in enumerate(w1_cols):
+            raw = sb("w1_raw%d" % n, [P, PACK, c1 - c0], F32)
+            nc.sync.dma_start(out=raw[:], in_=w1_rows[:, :, c0:c1])
+            w1_raw.append(raw)
+        load_vector(g1, gain1)
+        wg = sb("wg", [P, PACK, S], F32)
+        for q in range(4):
+            nc.sync.dma_start(out=wg[32 * q : 32 * q + 32, :, :], in_=wgs.rearrange("(r t) j -> r t j", t=PACK))
+        nc.sync.dma_start(lists[1][:], offs2)
+        page_rows = page0.rearrange("(b p t) c -> b t p c", b=2, t=PACK)
+        pages = []
+        for k, (b, t) in enumerate(slices):
+            page = sb("page%d" % k, [P, T2], F32)
+            nc.sync.dma_start(out=page[:], in_=page_rows[b, t])
+            pages.append(page)
+        nc.sync.dma_start(lists[2][:], offs3)
+        nc.sync.dma_start(lists[3][:], offs4)
+        load_vector(g2, gain2)
+        load_vector(bs, base)
+        w3_raw = {}
+        for a in range(2):
+            for b in range(2):
+                raw = sb("w3_raw%d%d" % (a, b), [P, PACK, PASS], F32)
+                rows = w3[a * PASS : (a + 1) * PASS, b * PASS : (b + 1) * PASS]
+                nc.sync.dma_start(out=raw[:], in_=rows.rearrange("(p i) c -> p i c", i=PACK))
+                w3_raw[a, b] = raw
+
+        w2d = sb("w2d", [P, 2 * 2 * H], U8)
+        w2sd = sb("w2sd", [P, 2 * H], U8)
+        nc.vector.tensor_copy(
+            out=w2d[:].bitcast(U16).rearrange("p (g t q) -> p g t q", g=4, t=PACK),
+            in_=w2_raw[:].bitcast(U16).rearrange("p a (b q t) -> p (a b) t q", b=2, t=PACK))
+
+        vw = sb("vw", [P, S], I32, tag="w2_raw")
+        vs = sb("vs", [P, S], U8)
+        nc.vector.tensor_copy(vw[:].bitcast(U32), tabw[:].bitcast(U32).indirect(lists[0][:]))
+        nc.vector.tensor_copy(vs[:], tabs[:].indirect(lists[0][:]))
+        nc.vector.tensor_copy(
+            out=w2sd[:].rearrange("p (g t q) -> p g t q", g=4, t=PACK),
+            in_=w2s_raw[:].rearrange("p a (b q t) -> p (a b) t q", b=2, t=PACK))
+
+        def round_and_deal(copy, grouped, raw, q0):
+            nq = raw.shape[2] // PACK
+            copy(out=grouped[:].rearrange("p (t q i) -> p q i t", t=PACK, i=PACK)[:, q0 : q0 + nq],
+                 in_=raw[:].rearrange("p i (q t) -> p q i t", t=PACK))
+
+        w1c = [sb("w1c%d" % b, [P, PASS], U32) for b in range(2)]
+        w1s = [sb("w1s%d" % b, [P, PASS], U8) for b in range(2)]
+        w1g = [sb("w1g%d" % b, [P, PASS * PACK], BF16) for b in range(2)]
+        for b in range(2):
+            round_and_deal(nc.scalar.copy, w1g[b], w1_raw[2 * b], 0)
+            round_and_deal(nc.vector.tensor_copy if b == 1 else nc.scalar.copy, w1g[b], w1_raw[2 * b + 1], 64)
+            quantize(w1c[b][:], w1s[b][:], w1g[b][:])
+
+        def first_product(dst, b, t, j0, n, start, stop):
+            cols = slice(t * P, (t + 1) * P)
+            nc.tensor.matmul_mx(out=dst, lhsT=w1c[b][:, cols].bitcast(FP8X4), lhsT_scale=w1s[b][:, cols],
+                                rhs=vw[:, j0 : j0 + n].bitcast(FP8X4), rhs_scale=vs[:, j0 : j0 + n],
+                                start=start, stop=stop)
+
+        bc = {(h, a): sb("bc%d%d" % (h, a), [P, HALF], U32) for h in range(2) for a in range(2)}
+        bsc = {(h, a): sb("bsc%d%d" % (h, a), [P, HALF], U8) for h in range(2) for a in range(2)}
+
+        for b in range(2):
+            for u in range(2):
+                acc = bank([P, PACK, QUART])
+                for t in range(PACK):
+                    first_product(acc[:, t, :], b, t, u * QUART, QUART, True, True)
+                act = sb("act%d%d" % (b, u), [P, QUART, PACK], F32)
+                nc.scalar.activation(out=act[:], in_=acc[:].rearrange("p t j -> p j t"), func=ACT.Gelu_apprx_tanh)
+                grouped = sb("bg%d%d" % (b, u), [P, QUART, PACK], BF16)
+                nc.vector.tensor_tensor(grouped[:], act[:], g1[:, b : b + 1, :].to_broadcast([P, QUART, PACK]), ALU.mult)
+                cols = slice(u * QUART, (u + 1) * QUART)
+                quantize(bc[0, b][:, cols], bsc[0, b][:, cols], grouped[:].rearrange("p j t -> p (j t)"))
+
+        def second_product(h, k, hs=None):
+            b, t = slices[k]
+            acc = bank([P, HALF])
+            for u in range(2):
+                cols = slice(u * QUART, (u + 1) * QUART)
+                first_product(acc[:, cols], b, t, h * HALF + u * QUART, QUART, True, False)
+                for a in range(2):
+                    c0 = ((2 * a + b) * PACK + t) * P
+                    nc.tensor.matmul_mx(out=acc[:, cols], lhsT=w2d[:, 2 * c0 : 2 * (c0 + P)].bitcast(FP4X4),
+                                        lhsT_scale=w2sd[:, c0 : c0 + P],
+                                        rhs=bc[h, a][:, cols].bitcast(FP8X4), rhs_scale=bsc[h, a][:, cols],
+                                        start=False, stop=(a == 1))
+            if hs is None:
+                hs = sb("hs%d%d" % (h, k), [P, HALF], F32)[:]
+            nc.scalar.copy(out=hs, in_=acc[:])
+            nc.vector.tensor_tensor(pages[k][:].indirect(lists[1][:, 16 * h : 16 * h + 16]), hs,
+                                    wg[:, t, h * HALF : (h + 1) * HALF], ALU.mult)
+            return hs
+
+        def interleave(grouped, rows):
+            nc.scalar.copy(out=grouped.rearrange("p (c i t) -> p c t i", i=PACK, t=PACK),
+                           in_=rows.rearrange("p t (c i) -> p c t i", i=PACK))
+
+        second_product(0, 0)
+        second_product(0, 1)
+        act1 = [sb("act1_%d" % b, [P, PACK, HALF], F32) for b in range(2)]
+        rows1 = [sb("rows1_%d" % b, [P, PACK, HALF], BF16) for b in range(2)]
+        for b in range(2):
+            for u in range(2):
+                acc = bank([P, 2, HALF])
+                for e in range(2):
+                    first_product(acc[:, e, :], b, 2 * u + e, HALF, HALF, True, True)
+                nc.scalar.activation(out=act1[b][:, 2 * u : 2 * u + 2, :], in_=acc[:], func=ACT.Gelu_apprx_tanh)
+        second_product(0, 2)
+        second_product(0, 3)
+        for b, t in slices:
+            nc.scalar.activation(out=rows1[b][:, t, :], in_=act1[b][:, t, :], func=ACT.Copy, scale=g1[:, b, t : t + 1])
+        second_product(0, 4)
+        second_product(0, 5)
+        for b in range(2):
+            grouped = sb("bg1_%d" % b, [P, HALF * PACK], BF16)
+            interleave(grouped[:], rows1[b][:])
+            quantize(bc[1, b][:], bsc[1, b][:], grouped[:])
+        second_product(0, 6)
+        last = second_product(0, 7)
+        nc.scalar.activation(out=warm[:, 2:3], in_=last[:, 0:1], func=ACT.Sin, scale=0.0)
+
+        picked = [sb("picked%d" % k, [P, NP], F32) for k in range(8)]
+        AHEAD = 3
+
+        def replace_and_pick(k):
+            second_product(1, k, picked[k - AHEAD][:, 0:HALF] if k >= AHEAD else None)
+            nc.vector.tensor_copy(picked[k][:], pages[k][:].indirect(lists[2][:]))
+
+        for k in range(AHEAD):
+            replace_and_pick(k)
+
+        w3g = {}
+        for a in range(2):
+            for b in range(2):
+                grouped = sb("w3g%d%d" % (a, b), [P, PASS * PACK], BF16, tag=("w1c0", "w1s0", "w1g0", "w1g1")[2 * a + b])
+                round_and_deal(nc.scalar.copy, grouped, w3_raw[a, b], 0)
+                w3g[a, b] = grouped
+        w3c, w3s = {}, {}
+
+        def quantize_w3(a):
+            w3c[a] = sb("w3c%d" % a, [P, H], U32, tag="picked%d" % (a + 1))
+            w3s[a] = sb("w3s%d" % a, [P, H], U8)
+            for b in range(2):
+                cols = slice(b * PASS, (b + 1) * PASS)
+                quantize(w3c[a][:, cols], w3s[a][:, cols], w3g[a, b][:])
+
+        flat = [raw[:].rearrange("p i c -> p (i c)") for raw in w1_raw]
+        work = [f[:, c : c + NP] for f in flat for c in range(0, f.shape[1], NP)]
+        ring = [w3_raw[1, 1][:, i, :] for i in range(2)]
+        xflat = [sb("xrows%d" % a, [P, 2 * NP], F32) for a in range(2)]
+        xrows = [x[:].bitcast(BF16).rearrange("p (t j) -> p t j", t=PACK) for x in xflat]
+        xg = [sb("xg%d" % a, [P, PACK * NP], BF16) for a in range(2)]
+        xc = [sb("xc%d" % a, [P, NP], U32) for a in range(2)]
+        xs = [sb("xs%d" % a, [P, NP], U8) for a in range(2)]
+        for k, (a, t) in enumerate(slices):
+            nc.scalar.activation(out=ring[k % 2], in_=picked[k][:], func=ACT.Abs)
+            if k + AHEAD < 8:
+                replace_and_pick(k + AHEAD)
+            if k in (1, 2):
+                quantize_w3(k - 1)
+            nc.scalar.activation(out=ring[k % 2], in_=ring[k % 2], func=ACT.Sin, scale=-1.0, bias=math.pi / 2)
+            nc.scalar.activation(out=xrows[a][:, t, :], in_=ring[k % 2], func=ACT.Copy, scale=g2[:, a, t : t + 1])
+            if t == PACK - 1:
+                interleave(xg[a][:], xrows[a])
+                quantize(xc[a][:], xs[a][:], xg[a][:])
+
+        slots = [picked[6][:], picked[7][:], ring[0], ring[1], xflat[1][:, 0:NP], xflat[1][:, NP : 2 * NP]]
+        out_rows = out.rearrange("(b p t) j -> b t p j", b=2, t=PACK)
+
+        def baseline(k):
+            nc.vector.tensor_copy(slots[k % 6], pages[k][:].indirect(lists[3][:]))
+
+        for k in range(6):
+            baseline(k)
+        for k, (b, t) in enumerate(slices):
+            acc = bank([P, NP])
+            cols = slice(b * PASS + t * P, b * PASS + (t + 1) * P)
+            for a in range(2):
+                nc.tensor.matmul_mx(out=acc[:], lhsT=w3c[a][:, cols].bitcast(FP8X4), lhsT_scale=w3s[a][:, cols],
+                                    rhs=xc[a][:].bitcast(FP8X4), rhs_scale=xs[a][:], start=(a == 0), stop=(a == 1))
+            diff = work[k]
+            nc.vector.scalar_tensor_tensor(diff, slots[k % 6], bs[:, b, t : t + 1], acc[:], ALU.mult, ALU.subtract)
+            if k + 6 < 8:
+                baseline(k + 6)
+            nc.scalar.activation(out=diff, in_=diff, func=ACT.Square)
+            nc.sync.dma_start(out=out_rows[b, t], in_=diff)

@@ -51,8 +51,10 @@ def tile_list_epoch_baseline_contrast_kernel(
         tabw = sb("tabw", [P, T], I32)
         tabs = sb("tabs", [P, T], U8)
         warm = sb("warm", [P, 4], F32)
-        nc.vector.memset(w2s_raw[:, 0, :].bitcast(I32), 0)
-        nc.gpsimd.memset(w2s_raw[:, 1, :].bitcast(I32), 0)
+        nc.gpsimd.memset(w2s_raw[:].bitcast(I32), 0)
+        for r in range(4):
+            nc.gpsimd.dma_start(out=w2s_raw[r:P:32, :, :].bitcast(I32),
+                                in_=w2_scales[:, r:16:4, :].rearrange("a q n -> q a n").bitcast(I32))
         nc.vector.memset(warm[:, 0:1], 0.0)
         nc.scalar.activation(out=warm[:, 1:2], in_=warm[:, 0:1], func=ACT.Gelu_apprx_tanh)
         g1 = sb("g1", [P, 2, PACK], F32)
@@ -62,27 +64,36 @@ def tile_list_epoch_baseline_contrast_kernel(
         def load_vector(tile, vec):
             nc.sync.dma_start(out=tile[:], in_=vec.rearrange("(b p t) -> p b t", b=2, t=PACK))
 
-        nc.sync.dma_start(out=w2_raw[:].bitcast(I32), in_=w2_words.rearrange("a p n -> p a n").bitcast(I32))
         nc.sync.dma_start(lists[0][:], offs)
+        nc.sync.dma_start(out=w2_raw[:].bitcast(I32), in_=w2_words.rearrange("a p n -> p a n").bitcast(I32))
+        nc.sync.dma_start(out=tabw[:], in_=tab_words[0].rearrange("p n i -> p (n i)").bitcast(I32))
         for q in range(4):
             rows = tab_scales[0, 4 * q : 4 * q + 4, :].bitcast(I32)
             nc.sync.dma_start(out=tabs[32 * q : 32 * q + 32, :].bitcast(I32),
                               in_=rows.unsqueeze(0).to_broadcast([8, 4, T // 4]))
-        nc.sync.dma_start(out=tabw[:], in_=tab_words[0].rearrange("p n i -> p (n i)").bitcast(I32))
-        for q in range(4):
-            nc.sync.dma_start(out=w2s_raw[32 * q : 32 * q + 4, :, :].bitcast(I32),
-                              in_=w2_scales[:, 4 * q : 4 * q + 4, :].rearrange("a r n -> r a n").bitcast(I32))
         w1_rows = w1.rearrange("(p i) c -> p i c", i=PACK)
-        w1_cols = [(c, c + 256) for c in range(0, H, 256)]
         w1_raw = []
-        for n, (c0, c1) in enumerate(w1_cols):
+        for n, (c0, c1) in enumerate([(0, 512), (512, 768), (768, 1024)]):
             raw = sb("w1_raw%d" % n, [P, PACK, c1 - c0], F32)
             nc.sync.dma_start(out=raw[:], in_=w1_rows[:, :, c0:c1])
             w1_raw.append(raw)
-        load_vector(g1, gain1)
-        wg = sb("wg", [P, PACK, S], F32)
-        for q in range(4):
-            nc.sync.dma_start(out=wg[32 * q : 32 * q + 32, :, :], in_=wgs.rearrange("(r t) j -> r t j", t=PACK))
+            if n == 0:
+                load_vector(g1, gain1)
+        wg = [sb("wg%d" % h, [P, PACK, HALF], F32) for h in range(2)]
+
+        def load_wg(h):
+            rows = wgs.rearrange("(r t) j -> r t j", t=PACK)[:, :, h * HALF : (h + 1) * HALF]
+            for q in range(4):
+                nc.sync.dma_start(out=wg[h][32 * q : 32 * q + 32, :, :], in_=rows)
+
+        w3_raw = {}
+
+        def load_w3(a, b):
+            w3_raw[a, b] = sb("w3_raw%d%d" % (a, b), [P, PACK, PASS], F32)
+            rows = w3[a * PASS : (a + 1) * PASS, b * PASS : (b + 1) * PASS]
+            nc.sync.dma_start(out=w3_raw[a, b][:], in_=rows.rearrange("(p i) c -> p i c", i=PACK))
+
+        load_wg(0)
         nc.sync.dma_start(lists[1][:], offs2)
         page_rows = page0.rearrange("(b p t) c -> b t p c", b=2, t=PACK)
         pages = []
@@ -90,17 +101,15 @@ def tile_list_epoch_baseline_contrast_kernel(
             page = sb("page%d" % k, [P, T2], F32)
             nc.sync.dma_start(out=page[:], in_=page_rows[b, t])
             pages.append(page)
+        load_w3(0, 0)
+        load_wg(1)
         nc.sync.dma_start(lists[2][:], offs3)
-        nc.sync.dma_start(lists[3][:], offs4)
+        load_w3(0, 1)
+        load_w3(1, 0)
+        load_w3(1, 1)
         load_vector(g2, gain2)
+        nc.sync.dma_start(lists[3][:], offs4)
         load_vector(bs, base)
-        w3_raw = {}
-        for a in range(2):
-            for b in range(2):
-                raw = sb("w3_raw%d%d" % (a, b), [P, PACK, PASS], F32)
-                rows = w3[a * PASS : (a + 1) * PASS, b * PASS : (b + 1) * PASS]
-                nc.sync.dma_start(out=raw[:], in_=rows.rearrange("(p i) c -> p i c", i=PACK))
-                w3_raw[a, b] = raw
 
         w2d = sb("w2d", [P, 2 * 2 * H], U8)
         w2sd = sb("w2sd", [P, 2 * H], U8)
@@ -119,14 +128,15 @@ def tile_list_epoch_baseline_contrast_kernel(
         def round_and_deal(copy, grouped, raw, q0):
             nq = raw.shape[2] // PACK
             copy(out=grouped[:].rearrange("p (t q i) -> p q i t", t=PACK, i=PACK)[:, q0 : q0 + nq],
-                 in_=raw[:].rearrange("p i (q t) -> p q i t", t=PACK))
+                 in_=raw.rearrange("p i (q t) -> p q i t", t=PACK))
 
         w1c = [sb("w1c%d" % b, [P, PASS], U32) for b in range(2)]
         w1s = [sb("w1s%d" % b, [P, PASS], U8) for b in range(2)]
         w1g = [sb("w1g%d" % b, [P, PASS * PACK], BF16) for b in range(2)]
         for b in range(2):
-            round_and_deal(nc.scalar.copy, w1g[b], w1_raw[2 * b], 0)
-            round_and_deal(nc.vector.tensor_copy if b == 1 else nc.scalar.copy, w1g[b], w1_raw[2 * b + 1], 64)
+            halves = (w1_raw[0][:, :, 0:256], w1_raw[0][:, :, 256:512]) if b == 0 else (w1_raw[1][:], w1_raw[2][:])
+            round_and_deal(nc.scalar.copy, w1g[b], halves[0], 0)
+            round_and_deal(nc.vector.tensor_copy, w1g[b], halves[1], 64)
             quantize(w1c[b][:], w1s[b][:], w1g[b][:])
 
         def first_product(dst, b, t, j0, n, start, stop):
@@ -153,20 +163,20 @@ def tile_list_epoch_baseline_contrast_kernel(
         def second_product(h, k, hs=None):
             b, t = slices[k]
             acc = bank([P, HALF])
-            for u in range(2):
-                cols = slice(u * QUART, (u + 1) * QUART)
-                first_product(acc[:, cols], b, t, h * HALF + u * QUART, QUART, True, False)
-                for a in range(2):
-                    c0 = ((2 * a + b) * PACK + t) * P
+            first_product(acc[:], b, t, h * HALF, HALF, True, False)
+            for a in range(2):
+                c0 = ((2 * a + b) * PACK + t) * P
+                for u in range(2):
+                    cols = slice(u * QUART, (u + 1) * QUART)
                     nc.tensor.matmul_mx(out=acc[:, cols], lhsT=w2d[:, 2 * c0 : 2 * (c0 + P)].bitcast(FP4X4),
                                         lhsT_scale=w2sd[:, c0 : c0 + P],
                                         rhs=bc[h, a][:, cols].bitcast(FP8X4), rhs_scale=bsc[h, a][:, cols],
-                                        start=False, stop=(a == 1))
+                                        start=False, stop=(a == 1 and u == 1))
             if hs is None:
                 hs = sb("hs%d%d" % (h, k), [P, HALF], F32)[:]
             nc.scalar.copy(out=hs, in_=acc[:])
             nc.vector.tensor_tensor(pages[k][:].indirect(lists[1][:, 16 * h : 16 * h + 16]), hs,
-                                    wg[:, t, h * HALF : (h + 1) * HALF], ALU.mult)
+                                    wg[h][:, t, :], ALU.mult)
             return hs
 
         def interleave(grouped, rows):
@@ -176,7 +186,6 @@ def tile_list_epoch_baseline_contrast_kernel(
         second_product(0, 0)
         second_product(0, 1)
         act1 = [sb("act1_%d" % b, [P, PACK, HALF], F32) for b in range(2)]
-        rows1 = [sb("rows1_%d" % b, [P, PACK, HALF], BF16) for b in range(2)]
         for b in range(2):
             for u in range(2):
                 acc = bank([P, 2, HALF])
@@ -185,6 +194,7 @@ def tile_list_epoch_baseline_contrast_kernel(
                 nc.scalar.activation(out=act1[b][:, 2 * u : 2 * u + 2, :], in_=acc[:], func=ACT.Gelu_apprx_tanh)
         second_product(0, 2)
         second_product(0, 3)
+        rows1 = [sb("rows1_%d" % b, [P, PACK, HALF], BF16, tag="hs0%d" % (2 * b)) for b in range(2)]
         for b, t in slices:
             nc.scalar.activation(out=rows1[b][:, t, :], in_=act1[b][:, t, :], func=ACT.Copy, scale=g1[:, b, t : t + 1])
         second_product(0, 4)
@@ -210,8 +220,8 @@ def tile_list_epoch_baseline_contrast_kernel(
         w3g = {}
         for a in range(2):
             for b in range(2):
-                grouped = sb("w3g%d%d" % (a, b), [P, PASS * PACK], BF16, tag=("w1c0", "w1s0", "w1g0", "w1g1")[2 * a + b])
-                round_and_deal(nc.scalar.copy, grouped, w3_raw[a, b], 0)
+                grouped = sb("w3g%d%d" % (a, b), [P, PASS * PACK], BF16, tag=("w3g00", "w1c0", "w1g0", "w1g1")[2 * a + b])
+                round_and_deal(nc.scalar.copy, grouped, w3_raw[a, b][:], 0)
                 w3g[a, b] = grouped
         w3c, w3s = {}, {}
 
@@ -250,12 +260,14 @@ def tile_list_epoch_baseline_contrast_kernel(
 
         for k in range(6):
             baseline(k)
-        for k, (b, t) in enumerate(slices):
-            acc = bank([P, NP])
-            cols = slice(b * PASS + t * P, b * PASS + (t + 1) * P)
-            for a in range(2):
-                nc.tensor.matmul_mx(out=acc[:], lhsT=w3c[a][:, cols].bitcast(FP8X4), lhsT_scale=w3s[a][:, cols],
+        accs = [bank([P, NP]) for k in range(8)]
+        for a in range(2):
+            for k in range(8):
+                cols = slice(k * P, (k + 1) * P)
+                nc.tensor.matmul_mx(out=accs[k][:], lhsT=w3c[a][:, cols].bitcast(FP8X4), lhsT_scale=w3s[a][:, cols],
                                     rhs=xc[a][:].bitcast(FP8X4), rhs_scale=xs[a][:], start=(a == 0), stop=(a == 1))
+        for k, (b, t) in enumerate(slices):
+            acc = accs[k]
             diff = work[k]
             nc.vector.scalar_tensor_tensor(diff, slots[k % 6], bs[:, b, t : t + 1], acc[:], ALU.mult, ALU.subtract)
             if k + 6 < 8:

@@ -2,6 +2,7 @@ import math
 from contextlib import ExitStack
 
 import concourse.mybir as mybir
+from concourse.masks import make_identity
 
 K, H, T, S, T2, NP = 512, 1024, 2048, 512, 1024, 512
 FLOPS = 2 * (2 * K * H * S + H * H * S + H * H * NP)
@@ -65,6 +66,8 @@ def tile_list_epoch_baseline_contrast_kernel(
             nc.sync.dma_start(out=tile[:], in_=vec.rearrange("(b p t) -> p b t", b=2, t=PACK))
 
         nc.sync.dma_start(lists[0][:], offs)
+        wg_raw = sb("wg_raw", [P, S], F32)
+        nc.sync.dma_start(out=wg_raw[:], in_=wgs)
         nc.sync.dma_start(out=w2_raw[:].bitcast(I32), in_=w2_words.rearrange("a p n -> p a n").bitcast(I32))
         nc.sync.dma_start(out=tabw[:], in_=tab_words[0].rearrange("p n i -> p (n i)").bitcast(I32))
         for q in range(4):
@@ -79,13 +82,6 @@ def tile_list_epoch_baseline_contrast_kernel(
             w1_raw.append(raw)
             if n == 0:
                 load_vector(g1, gain1)
-        wg = [sb("wg%d" % h, [P, PACK, HALF], F32) for h in range(2)]
-
-        def load_wg(h):
-            rows = wgs.rearrange("(r t) j -> r t j", t=PACK)[:, :, h * HALF : (h + 1) * HALF]
-            for q in range(4):
-                nc.sync.dma_start(out=wg[h][32 * q : 32 * q + 32, :, :], in_=rows)
-
         w3_raw = {}
 
         def load_w3(a, b):
@@ -93,7 +89,6 @@ def tile_list_epoch_baseline_contrast_kernel(
             rows = w3[a * PASS : (a + 1) * PASS, b * PASS : (b + 1) * PASS]
             nc.sync.dma_start(out=w3_raw[a, b][:], in_=rows.rearrange("(p i) c -> p i c", i=PACK))
 
-        load_wg(0)
         nc.sync.dma_start(lists[1][:], offs2)
         page_rows = page0.rearrange("(b p t) c -> b t p c", b=2, t=PACK)
         pages = []
@@ -101,15 +96,31 @@ def tile_list_epoch_baseline_contrast_kernel(
             page = sb("page%d" % k, [P, T2], F32)
             nc.sync.dma_start(out=page[:], in_=page_rows[b, t])
             pages.append(page)
-        load_w3(0, 0)
-        load_wg(1)
         nc.sync.dma_start(lists[2][:], offs3)
+        load_w3(0, 0)
         load_w3(0, 1)
         load_w3(1, 0)
         load_w3(1, 1)
         load_vector(g2, gain2)
         nc.sync.dma_start(lists[3][:], offs4)
         load_vector(bs, base)
+
+        ident = sb("ident", [P, P], F32)
+        make_identity(nc, ident[:])
+        turned = bank([P, PACK, P])
+        for c in range(PACK):
+            nc.tensor.transpose(turned[:, c, :], wg_raw[:, c * P : (c + 1) * P], ident[:])
+        wg = []
+        for t in range(PACK):
+            spread = sb("spread%d" % t, [P, PACK, PACK, 32], F32)
+            picks = turned[:].rearrange("p c (q t) -> p c t q", t=PACK)[:, :, t : t + 1, :]
+            nc.scalar.copy(out=spread[:], in_=picks.to_broadcast([P, PACK, PACK, 32]))
+            back = bank([P, S])
+            for c in range(PACK):
+                nc.tensor.transpose(back[:, c * P : (c + 1) * P], spread[:, c].rearrange("p r q -> p (r q)"), ident[:])
+            wgt = sb("wg%d" % t, [P, S], F32)
+            nc.scalar.copy(out=wgt[:], in_=back[:])
+            wg.append(wgt)
 
         w2d = sb("w2d", [P, 2 * 2 * H], U8)
         w2sd = sb("w2sd", [P, 2 * H], U8)
@@ -176,7 +187,7 @@ def tile_list_epoch_baseline_contrast_kernel(
                 hs = sb("hs%d%d" % (h, k), [P, HALF], F32)[:]
             nc.scalar.copy(out=hs, in_=acc[:])
             nc.vector.tensor_tensor(pages[k][:].indirect(lists[1][:, 16 * h : 16 * h + 16]), hs,
-                                    wg[h][:, t, :], ALU.mult)
+                                    wg[t][:, h * HALF : (h + 1) * HALF], ALU.mult)
             return hs
 
         def interleave(grouped, rows):

@@ -52,7 +52,9 @@ def tile_list_epoch_baseline_contrast_kernel(
         tabw = sb("tabw", [P, T], I32)
         tabs = sb("tabs", [P, T], U8)
         warm = sb("warm", [P, 4], F32)
-        nc.gpsimd.memset(w2s_raw[:].bitcast(I32), 0)
+        ident = sb("ident", [P, P], F32)
+        make_identity(nc, ident[:])
+        nc.vector.memset(w2s_raw[:].bitcast(I32), 0)
         for r in range(4):
             nc.gpsimd.dma_start(out=w2s_raw[r:P:32, :, :].bitcast(I32),
                                 in_=w2_scales[:, r:16:4, :].rearrange("a q n -> q a n").bitcast(I32))
@@ -105,8 +107,6 @@ def tile_list_epoch_baseline_contrast_kernel(
         nc.sync.dma_start(lists[3][:], offs4)
         load_vector(bs, base)
 
-        ident = sb("ident", [P, P], F32)
-        make_identity(nc, ident[:])
         turned = bank([P, PACK, P])
         for c in range(PACK):
             nc.tensor.transpose(turned[:, c, :], wg_raw[:, c * P : (c + 1) * P], ident[:])
@@ -123,15 +123,15 @@ def tile_list_epoch_baseline_contrast_kernel(
             wg.append(wgt)
 
         w2d = sb("w2d", [P, 2 * 2 * H], U8)
-        w2sd = sb("w2sd", [P, 2 * H], U8)
         nc.vector.tensor_copy(
             out=w2d[:].bitcast(U16).rearrange("p (g t q) -> p g t q", g=4, t=PACK),
             in_=w2_raw[:].bitcast(U16).rearrange("p a (b q t) -> p (a b) t q", b=2, t=PACK))
 
         vw = sb("vw", [P, S], I32, tag="w2_raw")
-        vs = sb("vs", [P, S], U8)
         nc.vector.tensor_copy(vw[:].bitcast(U32), tabw[:].bitcast(U32).indirect(lists[0][:]))
+        vs = sb("vs", [P, S], U8, tag="tabw")
         nc.vector.tensor_copy(vs[:], tabs[:].indirect(lists[0][:]))
+        w2sd = sb("w2sd", [P, 2 * H], U8, tag="tabs")
         nc.vector.tensor_copy(
             out=w2sd[:].rearrange("p (g t q) -> p g t q", g=4, t=PACK),
             in_=w2s_raw[:].rearrange("p a (b q t) -> p (a b) t q", b=2, t=PACK))
@@ -143,7 +143,7 @@ def tile_list_epoch_baseline_contrast_kernel(
 
         w1c = [sb("w1c%d" % b, [P, PASS], U32) for b in range(2)]
         w1s = [sb("w1s%d" % b, [P, PASS], U8) for b in range(2)]
-        w1g = [sb("w1g%d" % b, [P, PASS * PACK], BF16) for b in range(2)]
+        w1g = [sb("w1g%d" % b, [P, PASS * PACK], BF16, tag=("w1g0", "w2s_raw")[b]) for b in range(2)]
         for b in range(2):
             halves = (w1_raw[0][:, :, 0:256], w1_raw[0][:, :, 256:512]) if b == 0 else (w1_raw[1][:], w1_raw[2][:])
             round_and_deal(nc.scalar.copy, w1g[b], halves[0], 0)
@@ -229,15 +229,18 @@ def tile_list_epoch_baseline_contrast_kernel(
             replace_and_pick(k)
 
         w3g = {}
-        for a in range(2):
-            for b in range(2):
-                grouped = sb("w3g%d%d" % (a, b), [P, PASS * PACK], BF16, tag=("w3g00", "w1c0", "w1g0", "w1g1")[2 * a + b])
-                round_and_deal(nc.scalar.copy, grouped, w3_raw[a, b][:], 0)
-                w3g[a, b] = grouped
+
+        def round_w3(a, b, tag):
+            w3g[a, b] = sb("w3g%d%d" % (a, b), [P, PASS * PACK], BF16, tag=tag)
+            round_and_deal(nc.scalar.copy, w3g[a, b], w3_raw[a, b][:], 0)
+
+        round_w3(0, 0, "hs04")
+        round_w3(0, 1, "w1c0")
+        round_w3(1, 0, "w1c1")
         w3c, w3s = {}, {}
 
         def quantize_w3(a):
-            w3c[a] = sb("w3c%d" % a, [P, H], U32, tag="picked%d" % (a + 1))
+            w3c[a] = sb("w3c%d" % a, [P, H], U32, tag="picked%d" % (2 * a + 2))
             w3s[a] = sb("w3s%d" % a, [P, H], U8)
             for b in range(2):
                 cols = slice(b * PASS, (b + 1) * PASS)
@@ -245,20 +248,22 @@ def tile_list_epoch_baseline_contrast_kernel(
 
         flat = [raw[:].rearrange("p i c -> p (i c)") for raw in w1_raw]
         work = [f[:, c : c + NP] for f in flat for c in range(0, f.shape[1], NP)]
-        ring = [w3_raw[1, 1][:, i, :] for i in range(2)]
+        ring = [w3_raw[1, 0][:, i, :] for i in range(3)]
         xflat = [sb("xrows%d" % a, [P, 2 * NP], F32) for a in range(2)]
         xrows = [x[:].bitcast(BF16).rearrange("p (t j) -> p t j", t=PACK) for x in xflat]
         xg = [sb("xg%d" % a, [P, PACK * NP], BF16) for a in range(2)]
         xc = [sb("xc%d" % a, [P, NP], U32) for a in range(2)]
         xs = [sb("xs%d" % a, [P, NP], U8) for a in range(2)]
         for k, (a, t) in enumerate(slices):
-            nc.scalar.activation(out=ring[k % 2], in_=picked[k][:], func=ACT.Abs)
+            nc.scalar.activation(out=ring[k % 3], in_=picked[k][:], func=ACT.Abs)
             if k + AHEAD < 8:
                 replace_and_pick(k + AHEAD)
-            if k in (1, 2):
-                quantize_w3(k - 1)
-            nc.scalar.activation(out=ring[k % 2], in_=ring[k % 2], func=ACT.Sin, scale=-1.0, bias=math.pi / 2)
-            nc.scalar.activation(out=xrows[a][:, t, :], in_=ring[k % 2], func=ACT.Copy, scale=g2[:, a, t : t + 1])
+            if k == 0:
+                round_w3(1, 1, "picked0")
+            if k in (2, 4):
+                quantize_w3(k // 2 - 1)
+            nc.scalar.activation(out=ring[k % 3], in_=ring[k % 3], func=ACT.Sin, scale=-1.0, bias=math.pi / 2)
+            nc.scalar.activation(out=xrows[a][:, t, :], in_=ring[k % 3], func=ACT.Copy, scale=g2[:, a, t : t + 1])
             if t == PACK - 1:
                 interleave(xg[a][:], xrows[a])
                 quantize(xc[a][:], xs[a][:], xg[a][:])

import math
from contextlib import ExitStack

import concourse.mybir as mybir
from concourse.masks import make_identity

K, H, T, S, T2, NP = 512, 1024, 2048, 512, 1024, 512
FLOPS = 2 * (2 * K * H * S + H * H * S + H * H * NP)

F32 = mybir.dt.float32
BF16 = mybir.dt.bfloat16
I32 = mybir.dt.int32
U32 = mybir.dt.uint32
U16 = mybir.dt.uint16
U8 = mybir.dt.uint8
FP8X4 = mybir.dt.float8_e4m3fn_x4
FP4X4 = mybir.dt.float4_e2m1fn_x4
ACT = mybir.ActivationFunctionType
ALU = mybir.AluOpType

P = 128
PACK = 4
PASS = P * PACK
HALF = S // 2
QUART = P


def tile_list_epoch_baseline_contrast_kernel(
    tc, tab_words, tab_scales, w1, w2_words, w2_scales, w3, gain1, gain2, base, page0, wgs,
    offs, offs2, offs3, offs4, out,
):
    nc = tc.nc
    slices = [(b, t) for b in range(2) for t in range(PACK)]

    with ExitStack() as ctx:
        keep = ctx.enter_context(tc.tile_pool(name="keep", bufs=1))
        psum = ctx.enter_context(tc.psum_pool(name="psum", bufs=8))

        def sb(name, shape, dtype, tag=""):
            return keep.tile(shape, dtype, name=name, tag=tag or name, align_bytes=64)

        def bank(shape):
            return psum.tile(shape, F32, name="bank")

        def quantize(codes, scales, src):
            nc.vector.quantize_mx(out=codes.bitcast(FP8X4), scales=scales, in_=src)

        lists = [keep.tile([P, S // 16], U16, name="list%d" % i) for i in range(4)]

        w2_raw = sb("w2_raw", [P, 2, 2 * H], U8)
        w2s_raw = sb("w2s_raw", [P, 2, H], U8)
        tabw = sb("tabw", [P, T], I32)
        tabs = sb("tabs", [P, T], U8)
        warm = sb("warm", [P, 4], F32)
        ident = sb("ident", [P, P], F32)
        make_identity(nc, ident[:])
        nc.vector.memset(w2s_raw[:].bitcast(I32), 0)
        for r in range(4):
            nc.gpsimd.dma_start(out=w2s_raw[r:P:32, :, :].bitcast(I32),
                                in_=w2_scales[:, r:16:4, :].rearrange("a q n -> q a n").bitcast(I32))
        nc.vector.memset(warm[:, 0:1], 0.0)
        nc.scalar.activation(out=warm[:, 1:2], in_=warm[:, 0:1], func=ACT.Gelu_apprx_tanh)
        g1 = sb("g1", [P, 2, PACK], F32)
        g2 = sb("g2", [P, 2, PACK], F32)
        bs = sb("bs", [P, 2, PACK], F32)

        def load_vector(tile, vec):
            nc.sync.dma_start(out=tile[:], in_=vec.rearrange("(b p t) -> p b t", b=2, t=PACK))

        nc.sync.dma_start(lists[0][:], offs)
        wg_raw = sb("wg_raw", [P, S], F32)
        nc.sync.dma_start(out=wg_raw[:], in_=wgs)
        nc.sync.dma_start(out=w2_raw[:].bitcast(I32), in_=w2_words.rearrange("a p n -> p a n").bitcast(I32))
        nc.sync.dma_start(out=tabw[:], in_=tab_words[0].rearrange("p n i -> p (n i)").bitcast(I32))
        for q in range(4):
            rows = tab_scales[0, 4 * q : 4 * q + 4, :].bitcast(I32)
            nc.sync.dma_start(out=tabs[32 * q : 32 * q + 32, :].bitcast(I32),
                              in_=rows.unsqueeze(0).to_broadcast([8, 4, T // 4]))
        w1_rows = w1.rearrange("(p i) c -> p i c", i=PACK)
        w1_raw = []
        for n, (c0, c1) in enumerate([(0, 512), (512, 768), (768, 1024)]):
            raw = sb("w1_raw%d" % n, [P, PACK, c1 - c0], F32)
            nc.sync.dma_start(out=raw[:], in_=w1_rows[:, :, c0:c1])
            w1_raw.append(raw)
            if n == 0:
                load_vector(g1, gain1)
        w3_raw = {}

        def load_w3(a, b):
            w3_raw[a, b] = sb("w3_raw%d%d" % (a, b), [P, PACK, PASS], F32)
            rows = w3[a * PASS : (a + 1) * PASS, b * PASS : (b + 1) * PASS]
            nc.sync.dma_start(out=w3_raw[a, b][:], in_=rows.rearrange("(p i) c -> p i c", i=PACK))

        nc.sync.dma_start(lists[1][:], offs2)
        page_rows = page0.rearrange("(b p t) c -> b t p c", b=2, t=PACK)
        pages = []
        for k, (b, t) in enumerate(slices):
            page = sb("page%d" % k, [P, T2], F32)
            nc.sync.dma_start(out=page[:], in_=page_rows[b, t])
            pages.append(page)
        nc.sync.dma_start(lists[2][:], offs3)
        load_w3(0, 0)
        load_w3(0, 1)
        load_w3(1, 0)
        load_w3(1, 1)
        load_vector(g2, gain2)
        nc.sync.dma_start(lists[3][:], offs4)
        load_vector(bs, base)

        turned = bank([P, PACK, P])
        for c in range(PACK):
            nc.tensor.transpose(turned[:, c, :], wg_raw[:, c * P : (c + 1) * P], ident[:])
        wg = []
        for t in range(PACK):
            spread = sb("spread%d" % t, [P, PACK, PACK, 32], F32)
            picks = turned[:].rearrange("p c (q t) -> p c t q", t=PACK)[:, :, t : t + 1, :]
            nc.scalar.copy(out=spread[:], in_=picks.to_broadcast([P, PACK, PACK, 32]))
            back = bank([P, S])
            for c in range(PACK):
                nc.tensor.transpose(back[:, c * P : (c + 1) * P], spread[:, c].rearrange("p r q -> p (r q)"), ident[:])
            wgt = sb("wg%d" % t, [P, S], F32)
            nc.scalar.copy(out=wgt[:], in_=back[:])
            wg.append(wgt)

        w2d = sb("w2d", [P, 2 * 2 * H], U8)
        nc.vector.tensor_copy(
            out=w2d[:].bitcast(U16).rearrange("p (g t q) -> p g t q", g=4, t=PACK),
            in_=w2_raw[:].bitcast(U16).rearrange("p a (b q t) -> p (a b) t q", b=2, t=PACK))

        vw = sb("vw", [P, S], I32, tag="w2_raw")
        nc.vector.tensor_copy(vw[:].bitcast(U32), tabw[:].bitcast(U32).indirect(lists[0][:]))
        vs = sb("vs", [P, S], U8, tag="tabw")
        nc.vector.tensor_copy(vs[:], tabs[:].indirect(lists[0][:]))
        w2sd = sb("w2sd", [P, 2 * H], U8, tag="tabs")
        nc.vector.tensor_copy(
            out=w2sd[:].rearrange("p (g t q) -> p g t q", g=4, t=PACK),
            in_=w2s_raw[:].rearrange("p a (b q t) -> p (a b) t q", b=2, t=PACK))

        def round_and_deal(copy, grouped, raw, q0):
            nq = raw.shape[2] // PACK
            copy(out=grouped[:].rearrange("p (t q i) -> p q i t", t=PACK, i=PACK)[:, q0 : q0 + nq],
                 in_=raw.rearrange("p i (q t) -> p q i t", t=PACK))

        w1c = [sb("w1c%d" % b, [P, PASS], U32) for b in range(2)]
        w1s = [sb("w1s%d" % b, [P, PASS], U8) for b in range(2)]
        w1g = [sb("w1g%d" % b, [P, PASS * PACK], BF16, tag=("w1g0", "w2s_raw")[b]) for b in range(2)]
        for b in range(2):
            halves = (w1_raw[0][:, :, 0:256], w1_raw[0][:, :, 256:512]) if b == 0 else (w1_raw[1][:], w1_raw[2][:])
            round_and_deal(nc.scalar.copy, w1g[b], halves[0], 0)
            round_and_deal(nc.vector.tensor_copy, w1g[b], halves[1], 64)
            quantize(w1c[b][:], w1s[b][:], w1g[b][:])

        def first_product(dst, b, t, j0, n, start, stop):
            cols = slice(t * P, (t + 1) * P)
            nc.tensor.matmul_mx(out=dst, lhsT=w1c[b][:, cols].bitcast(FP8X4), lhsT_scale=w1s[b][:, cols],
                                rhs=vw[:, j0 : j0 + n].bitcast(FP8X4), rhs_scale=vs[:, j0 : j0 + n],
                                start=start, stop=stop)

        bc = {(h, a): sb("bc%d%d" % (h, a), [P, HALF], U32) for h in range(2) for a in range(2)}
        bsc = {(h, a): sb("bsc%d%d" % (h, a), [P, HALF], U8) for h in range(2) for a in range(2)}

        for b in range(2):
            for u in range(2):
                acc = bank([P, PACK, QUART])
                for t in range(PACK):
                    first_product(acc[:, t, :], b, t, u * QUART, QUART, True, True)
                act = sb("act%d%d" % (b, u), [P, QUART, PACK], F32)
                nc.scalar.activation(out=act[:], in_=acc[:].rearrange("p t j -> p j t"), func=ACT.Gelu_apprx_tanh)
                grouped = sb("bg%d%d" % (b, u), [P, QUART, PACK], BF16)
                nc.vector.tensor_tensor(grouped[:], act[:], g1[:, b : b + 1, :].to_broadcast([P, QUART, PACK]), ALU.mult)
                cols = slice(u * QUART, (u + 1) * QUART)
                quantize(bc[0, b][:, cols], bsc[0, b][:, cols], grouped[:].rearrange("p j t -> p (j t)"))

        def second_product(h, k, hs=None):
            b, t = slices[k]
            acc = bank([P, HALF])
            first_product(acc[:], b, t, h * HALF, HALF, True, False)
            for a in range(2):
                c0 = ((2 * a + b) * PACK + t) * P
                for u in range(2):
                    cols = slice(u * QUART, (u + 1) * QUART)
                    nc.tensor.matmul_mx(out=acc[:, cols], lhsT=w2d[:, 2 * c0 : 2 * (c0 + P)].bitcast(FP4X4),
                                        lhsT_scale=w2sd[:, c0 : c0 + P],
                                        rhs=bc[h, a][:, cols].bitcast(FP8X4), rhs_scale=bsc[h, a][:, cols],
                                        start=False, stop=(a == 1 and u == 1))
            if hs is None:
                hs = sb("hs%d%d" % (h, k), [P, HALF], F32)[:]
            nc.scalar.copy(out=hs, in_=acc[:])
            nc.vector.tensor_tensor(pages[k][:].indirect(lists[1][:, 16 * h : 16 * h + 16]), hs,
                                    wg[t][:, h * HALF : (h + 1) * HALF], ALU.mult)
            return hs

        def interleave(grouped, rows):
            nc.scalar.copy(out=grouped.rearrange("p (c i t) -> p c t i", i=PACK, t=PACK),
                           in_=rows.rearrange("p t (c i) -> p c t i", i=PACK))

        second_product(0, 0)
        second_product(0, 1)
        act1 = [sb("act1_%d" % b, [P, PACK, HALF], F32) for b in range(2)]
        for b in range(2):
            for u in range(2):
                acc = bank([P, 2, HALF])
                for e in range(2):
                    first_product(acc[:, e, :], b, 2 * u + e, HALF, HALF, True, True)
                nc.scalar.activation(out=act1[b][:, 2 * u : 2 * u + 2, :], in_=acc[:], func=ACT.Gelu_apprx_tanh)
        second_product(0, 2)
        second_product(0, 3)
        rows1 = [sb("rows1_%d" % b, [P, PACK, HALF], BF16, tag="hs0%d" % (2 * b)) for b in range(2)]
        for b, t in slices:
            nc.scalar.activation(out=rows1[b][:, t, :], in_=act1[b][:, t, :], func=ACT.Copy, scale=g1[:, b, t : t + 1])
        second_product(0, 4)
        second_product(0, 5)
        for b in range(2):
            grouped = sb("bg1_%d" % b, [P, HALF * PACK], BF16)
            interleave(grouped[:], rows1[b][:])
            quantize(bc[1, b][:], bsc[1, b][:], grouped[:])
        second_product(0, 6)
        last = second_product(0, 7)
        nc.scalar.activation(out=warm[:, 2:3], in_=last[:, 0:1], func=ACT.Sin, scale=0.0)

        picked = [sb("picked%d" % k, [P, NP], F32) for k in range(8)]
        AHEAD = 3

        def replace_and_pick(k):
            second_product(1, k, picked[k - AHEAD][:, 0:HALF] if k >= AHEAD else None)
            nc.vector.tensor_copy(picked[k][:], pages[k][:].indirect(lists[2][:]))

        for k in range(AHEAD):
            replace_and_pick(k)

        w3g = {}

        def round_w3(a, b, tag):
            w3g[a, b] = sb("w3g%d%d" % (a, b), [P, PASS * PACK], BF16, tag=tag)
            round_and_deal(nc.scalar.copy, w3g[a, b], w3_raw[a, b][:], 0)

        round_w3(0, 0, "hs04")
        round_w3(0, 1, "w1c0")
        round_w3(1, 0, "w1c1")
        w3c, w3s = {}, {}

        def quantize_w3(a):
            w3c[a] = sb("w3c%d" % a, [P, H], U32, tag="picked%d" % (2 * a + 2))
            w3s[a] = sb("w3s%d" % a, [P, H], U8)
            for b in range(2):
                cols = slice(b * PASS, (b + 1) * PASS)
                quantize(w3c[a][:, cols], w3s[a][:, cols], w3g[a, b][:])

        flat = [raw[:].rearrange("p i c -> p (i c)") for raw in w1_raw]
        work = [f[:, c : c + NP] for f in flat for c in range(0, f.shape[1], NP)]
        ring = [w3_raw[1, 0][:, i, :] for i in range(3)]
        xflat = [sb("xrows%d" % a, [P, 2 * NP], F32) for a in range(2)]
        xrows = [x[:].bitcast(BF16).rearrange("p (t j) -> p t j", t=PACK) for x in xflat]
        xg = [sb("xg%d" % a, [P, PACK * NP], BF16) for a in range(2)]
        xc = [sb("xc%d" % a, [P, NP], U32) for a in range(2)]
        xs = [sb("xs%d" % a, [P, NP], U8) for a in range(2)]
        for k, (a, t) in enumerate(slices):
            nc.scalar.activation(out=ring[k % 3], in_=picked[k][:], func=ACT.Abs)
            if k + AHEAD < 8:
                replace_and_pick(k + AHEAD)
            if k == 0:
                round_w3(1, 1, "picked0")
            if k in (2, 4):
                quantize_w3(k // 2 - 1)
            nc.scalar.activation(out=ring[k % 3], in_=ring[k % 3], func=ACT.Sin, scale=-1.0, bias=math.pi / 2)
            nc.scalar.activation(out=xrows[a][:, t, :], in_=ring[k % 3], func=ACT.Copy, scale=g2[:, a, t : t + 1])
            if t == PACK - 1:
                interleave(xg[a][:], xrows[a])
                quantize(xc[a][:], xs[a][:], xg[a][:])

        slots = [picked[6][:], picked[7][:], ring[0], ring[1], xflat[1][:, 0:NP], xflat[1][:, NP : 2 * NP]]
        out_rows = out.rearrange("(b p t) j -> b t p j", b=2, t=PACK)

        def baseline(k):
            nc.vector.tensor_copy(slots[k % 6], pages[k][:].indirect(lists[3][:]))

        for k in range(6):
            baseline(k)
        accs = [bank([P, NP]) for k in range(8)]
        for a in range(2):
            for k in range(8):
                cols = slice(k * P, (k + 1) * P)
                nc.tensor.matmul_mx(out=accs[k][:], lhsT=w3c[a][:, cols].bitcast(FP8X4), lhsT_scale=w3s[a][:, cols],
                                    rhs=xc[a][:].bitcast(FP8X4), rhs_scale=xs[a][:], start=(a == 0), stop=(a == 1))
        for k, (b, t) in enumerate(slices):
            acc = accs[k]
            diff = work[k]
            nc.vector.scalar_tensor_tensor(diff, slots[k % 6], bs[:, b, t : t + 1], acc[:], ALU.mult, ALU.subtract)
            if k + 6 < 8:
                baseline(k + 6)
            nc.scalar.activation(out=diff, in_=diff, func=ACT.Square)
            nc.sync.dma_start(out=out_rows[b, t], in_=diff)
